import numpy as np
import ml_dtypes


def mxq(x, axis, fmt="e4m3"):
    dtype, down = {"e4m3": (ml_dtypes.float8_e4m3fn, 7), "e5m2": (ml_dtypes.float8_e5m2, 14)}[fmt]
    v = np.moveaxis(np.asarray(x, np.float32).astype(ml_dtypes.bfloat16).astype(np.float64), axis, -1)
    blocks = v.reshape(v.shape[:-1] + (-1, 32))
    amax = np.abs(blocks).max(-1, keepdims=True)
    byte = np.maximum(np.where(amax > 0, np.frexp(amax)[1] - 1 + 127, 0) - down, 1)
    scale = np.exp2(byte - 127.0)
    codes = (blocks / scale).astype(np.float32).astype(dtype).astype(np.float64)
    return np.moveaxis((codes * scale).reshape(v.shape), -1, axis)


WIDE = False


def mx_kscale(k):
    if not WIDE:
        return np.ones(k)
    levels = np.array([10, -10, 5, -5, 0])
    if k % 512:
        return np.exp2(np.random.permutation(np.resize(levels, k // 32))).repeat(32)
    a = np.empty((k // 512, 16))
    for p in range(k // 512):
        a[p, :8] = np.random.permutation(np.resize(levels, 8))
        for g in range(8):
            far = levels[np.abs(levels - a[p, g]) >= 10]
            a[p, g + 8] = far[np.random.randint(len(far))]
    return np.exp2(a.ravel()).repeat(32)


def f64(x):
    return np.asarray(x).astype(np.float64)


def striped(idx):
    return np.tile(idx.reshape(-1, 16).T, (8, 1)).astype(np.uint16)


def unstriped(offs):
    return offs[:16].T.reshape(-1).astype(np.int64)


K, T, S, N = 512, 2048, 1024, 512


def setup_inputs():
    n = np.random.standard_normal
    s = mx_kscale(K)[:, None]
    return {
        "xT": (n((K, S)) * s).astype(np.float32),
        "w": (n((K, N)) / np.sqrt(K) / s).astype(np.float32),
        "gate": np.tile(np.random.uniform(0.2, 1.0, S), (N, 1)).astype(np.float32),
        "offs": striped(np.sort(np.random.permutation(T)[:S])),
    }


def reference(xT, w, gate, offs):
    idx = unstriped(offs)
    xq = mxq(f64(xT), 0, "e4m3")
    y = mxq(f64(w), 0, "e4m3").T @ xq
    out = np.zeros((N, T))
    out[:, idx] = f64(gate) * y
    return out

@@ -1,0 +1,144 @@
+from contextlib import ExitStack
+
+import concourse.mybir as mybir
+
+K, T, S, N = 512, 2048, 1024, 512
+P = 128
+PACK = 4
+FLOPS = 2 * K * S * N
+BYTES = 4 * (K * S + K * N + S + N * T) + 2 * S
+
+F32 = mybir.dt.float32
+BF16 = mybir.dt.bfloat16
+U32 = mybir.dt.uint32
+U16 = mybir.dt.uint16
+U8 = mybir.dt.uint8
+FP8X4 = mybir.dt.float8_e4m3fn_x4
+MULT = mybir.AluOpType.mult
+
+
+def interleave(copy, dst, src):
+    copy(
+        out=dst.rearrange("p (c i j) -> p c j i", i=4, j=PACK),
+        in_=src.rearrange("p j (c i) -> p c j i", i=4),
+    )
+
+
+def tile_picked_place_lin_none_srt_l_kernel(tc, xT, w, gate, offs, out):
+    nc = tc.nc
+    Q = 256
+    nq = S // Q
+    x_rows = xT.rearrange("(p j) s -> p j s", j=PACK)
+    w_rows = w.rearrange("(p j) n -> p j n", j=PACK)
+
+    with ExitStack() as ctx:
+        keep = ctx.enter_context(tc.tile_pool(name="keep", bufs=1))
+        psum = ctx.enter_context(tc.psum_pool(name="psum", bufs=1))
+
+        offsets = keep.tile([P, S // 16], U16, name="offsets")
+        gates = keep.tile([P, S], F32, name="gates", align_bytes=64)
+        x_raw = [keep.tile([P, PACK, Q], F32, name=f"x_raw{q}") for q in range(nq)]
+        w_raw = [keep.tile([P, PACK, 256], F32, name=f"w_raw{h}") for h in range(2)]
+        x_grp = [keep.tile([P, PACK * Q], BF16, name=f"x_grp{q}", align_bytes=64) for q in range(nq)]
+        w_grp = [keep.tile([P, PACK * 256], BF16, name=f"w_grp{h}", align_bytes=64) for h in range(2)]
+        x_codes = keep.tile([P, S], U32, name="x_codes", align_bytes=64)
+        x_scales = keep.tile([P, S], U8, name="x_scales", align_bytes=64)
+        w_codes = keep.tile([P, N], U32, name="w_codes", align_bytes=64)
+        w_scales = keep.tile([P, N], U8, name="w_scales", align_bytes=64)
+        windows = [keep.tile([P, T], F32, name=f"window{m}") for m in range(4)]
+        ys = [keep.tile([P, S], F32, name=f"y{m}", align_bytes=64) for m in range(4)]
+
+        def load_x(q):
+            nc.sync.dma_start(out=x_raw[q][:], in_=x_rows[:, :, q * Q : (q + 1) * Q])
+
+        def load_w(h):
+            nc.sync.dma_start(out=w_raw[h][:], in_=w_rows[:, :, h * 256 : (h + 1) * 256])
+
+        load_w(0)
+        load_x(0)
+        nc.sync.dma_start(offsets[:], offs)
+        nc.sync.dma_start(out=gates[:, 0:Q], in_=gate[0:P, 0:Q])
+        load_x(1)
+        nc.sync.dma_start(out=gates[:, Q:S], in_=gate[0:P, Q:S])
+        load_x(2)
+        load_x(3)
+        load_w(1)
+
+        for m in range(2):
+            nc.vector.memset(windows[m][:], 0.0)
+        for m in range(2, 4):
+            nc.gpsimd.memset(windows[m][:], 0.0)
+
+        def quantise_w(h):
+            nc.vector.quantize_mx(
+                out=w_codes[:, h * 256 : (h + 1) * 256].bitcast(FP8X4),
+                scales=w_scales[:, h * 256 : (h + 1) * 256],
+                in_=w_grp[h][:],
+            )
+
+        def quantise_x(q):
+            nc.vector.quantize_mx(
+                out=x_codes[:, q * Q : (q + 1) * Q].bitcast(FP8X4),
+                scales=x_scales[:, q * Q : (q + 1) * Q],
+                in_=x_grp[q][:],
+            )
+
+        def product(m, j0, j1, bank):
+            acc = psum.tile([P, 512], F32, name=f"bank{bank}")
+            nc.tensor.matmul_mx(
+                out=acc[:, 0 : j1 - j0],
+                lhsT=w_codes[:, m * P : (m + 1) * P].bitcast(FP8X4),
+                lhsT_scale=w_scales[:, m * P : (m + 1) * P],
+                rhs=x_codes[:, j0:j1].bitcast(FP8X4),
+                rhs_scale=x_scales[:, j0:j1],
+                start=True,
+                stop=True,
+            )
+            nc.scalar.copy(out=ys[m][:, j0:j1], in_=acc[:, 0 : j1 - j0])
+
+        def scatter(m, j0, j1):
+            nc.vector.tensor_tensor(
+                windows[m][:].indirect(offsets[:, j0 // 16 : j1 // 16]), ys[m][:, j0:j1], gates[:, j0:j1], MULT
+            )
+
+        def store(m):
+            nc.sync.dma_start(out=out[m * P : (m + 1) * P, :], in_=windows[m][:])
+
+        interleave(nc.scalar.copy, w_grp[0][:], w_raw[0][:])
+        interleave(nc.vector.tensor_copy, x_grp[0][:], x_raw[0][:])
+        quantise_w(0)
+        quantise_x(0)
+        product(0, 0, Q, 0)
+        product(1, 0, Q, 1)
+        interleave(nc.vector.tensor_copy, x_grp[1][:], x_raw[1][:])
+        scatter(0, 0, Q)
+        quantise_x(1)
+        product(0, Q, 2 * Q, 2)
+        product(1, Q, 2 * Q, 3)
+        interleave(nc.scalar.copy, x_grp[2][:], x_raw[2][:])
+        scatter(1, 0, Q)
+        quantise_x(2)
+        product(0, 2 * Q, 3 * Q, 4)
+        product(1, 2 * Q, 3 * Q, 5)
+        interleave(nc.scalar.copy, x_grp[3][:], x_raw[3][:])
+        scatter(0, Q, 2 * Q)
+        scatter(1, Q, 2 * Q)
+        quantise_x(3)
+        product(0, 3 * Q, S, 6)
+        product(1, 3 * Q, S, 7)
+        interleave(nc.scalar.copy, w_grp[1][:], w_raw[1][:])
+        scatter(0, 2 * Q, 3 * Q)
+        scatter(1, 2 * Q, 3 * Q)
+        quantise_w(1)
+        scatter(0, 3 * Q, S)
+        store(0)
+        product(2, 0, 512, 0)
+        product(2, 512, S, 1)
+        scatter(1, 3 * Q, S)
+        store(1)
+        product(3, 0, 512, 2)
+        product(3, 512, S, 3)
+        scatter(2, 0, S)
+        store(2)
+        scatter(3, 0, S)
+        store(3)

@@ -26,8 +26,6 @@ def interleave(copy, dst, src):
 
 def tile_picked_place_lin_none_srt_l_kernel(tc, xT, w, gate, offs, out):
     nc = tc.nc
-    Q = 256
-    nq = S // Q
     x_rows = xT.rearrange("(p j) s -> p j s", j=PACK)
     w_rows = w.rearrange("(p j) n -> p j n", j=PACK)
 
@@ -35,58 +33,72 @@ def tile_picked_place_lin_none_srt_l_kernel(tc, xT, w, gate, offs, out):
         keep = ctx.enter_context(tc.tile_pool(name="keep", bufs=1))
         psum = ctx.enter_context(tc.psum_pool(name="psum", bufs=1))
 
+        x_cuts = [(0, 256), (256, 512), (512, 768), (768, 1024)]
+        w_cuts = [(0, 128), (128, 256), (256, 512)]
         offsets = keep.tile([P, S // 16], U16, name="offsets")
         gates = keep.tile([P, S], F32, name="gates", align_bytes=64)
-        x_raw = [keep.tile([P, PACK, Q], F32, name=f"x_raw{q}") for q in range(nq)]
-        w_raw = [keep.tile([P, PACK, 256], F32, name=f"w_raw{h}") for h in range(2)]
-        x_grp = [keep.tile([P, PACK * Q], BF16, name=f"x_grp{q}", align_bytes=64) for q in range(nq)]
-        w_grp = [keep.tile([P, PACK * 256], BF16, name=f"w_grp{h}", align_bytes=64) for h in range(2)]
+        x_raw = [keep.tile([P, PACK, b - a], F32, name=f"x_raw{a}") for a, b in x_cuts]
+        w_raw = [keep.tile([P, PACK, b - a], F32, name=f"w_raw{a}") for a, b in w_cuts]
+        x_grp = [keep.tile([P, PACK * (b - a)], BF16, name=f"x_grp{a}", align_bytes=64) for a, b in x_cuts]
+        w_grp = [keep.tile([P, PACK * (b - a)], BF16, name=f"w_grp{a}", align_bytes=64) for a, b in w_cuts]
         x_codes = keep.tile([P, S], U32, name="x_codes", align_bytes=64)
         x_scales = keep.tile([P, S], U8, name="x_scales", align_bytes=64)
         w_codes = keep.tile([P, N], U32, name="w_codes", align_bytes=64)
         w_scales = keep.tile([P, N], U8, name="w_scales", align_bytes=64)
         windows = [keep.tile([P, T], F32, name=f"window{m}") for m in range(4)]
         ys = [keep.tile([P, S], F32, name=f"y{m}", align_bytes=64) for m in range(4)]
+        zero = keep.tile([P, 8], F32, name="zero")
 
-        def load_x(q):
-            nc.sync.dma_start(out=x_raw[q][:], in_=x_rows[:, :, q * Q : (q + 1) * Q])
+        def load_x(i):
+            a, b = x_cuts[i]
+            nc.sync.dma_start(out=x_raw[i][:], in_=x_rows[:, :, a:b])
 
-        def load_w(h):
-            nc.sync.dma_start(out=w_raw[h][:], in_=w_rows[:, :, h * 256 : (h + 1) * 256])
+        def load_w(i):
+            a, b = w_cuts[i]
+            nc.sync.dma_start(out=w_raw[i][:], in_=w_rows[:, :, a:b])
+
+        def load_gate(a, b):
+            nc.sync.dma_start(out=gates[:, a:b], in_=gate[0:P, a:b])
 
         load_w(0)
         load_x(0)
         nc.sync.dma_start(offsets[:], offs)
-        nc.sync.dma_start(out=gates[:, 0:Q], in_=gate[0:P, 0:Q])
+        load_gate(0, 256)
+        load_w(1)
         load_x(1)
-        nc.sync.dma_start(out=gates[:, Q:S], in_=gate[0:P, Q:S])
+        load_w(2)
+        load_gate(256, 1024)
         load_x(2)
         load_x(3)
-        load_w(1)
 
-        for m in range(2):
+        nc.vector.memset(zero[:], 0.0)
+        for m in range(3):
             nc.vector.memset(windows[m][:], 0.0)
-        for m in range(2, 4):
-            nc.gpsimd.memset(windows[m][:], 0.0)
+        nc.scalar.copy(out=windows[3][:], in_=zero[:, 0:1].to_broadcast([P, T]))
 
-        def quantise_w(h):
+        def group(copy, grp, raw, a, b):
+            interleave(copy, grp[:, PACK * a : PACK * b], raw[:, :, a:b])
+
+        def quantise_w(i):
+            a, b = w_cuts[i]
             nc.vector.quantize_mx(
-                out=w_codes[:, h * 256 : (h + 1) * 256].bitcast(FP8X4),
-                scales=w_scales[:, h * 256 : (h + 1) * 256],
-                in_=w_grp[h][:],
+                out=w_codes[:, a:b].bitcast(FP8X4), scales=w_scales[:, a:b], in_=w_grp[i][:]
             )
 
-        def quantise_x(q):
+        def quantise_x(i):
+            a, b = x_cuts[i]
             nc.vector.quantize_mx(
-                out=x_codes[:, q * Q : (q + 1) * Q].bitcast(FP8X4),
-                scales=x_scales[:, q * Q : (q + 1) * Q],
-                in_=x_grp[q][:],
+                out=x_codes[:, a:b].bitcast(FP8X4), scales=x_scales[:, a:b], in_=x_grp[i][:]
             )
 
-        def product(m, j0, j1, bank):
-            acc = psum.tile([P, 512], F32, name=f"bank{bank}")
+        banks = [psum.tile([P, 512], F32, name=f"bank{b}") for b in range(8)]
+        free = list(range(11))
+
+        def product(m, j0, j1):
+            acc = banks[free[0] % 8][:, 0 : j1 - j0]
+            free.remove(free[0])
             nc.tensor.matmul_mx(
-                out=acc[:, 0 : j1 - j0],
+                out=acc,
                 lhsT=w_codes[:, m * P : (m + 1) * P].bitcast(FP8X4),
                 lhsT_scale=w_scales[:, m * P : (m + 1) * P],
                 rhs=x_codes[:, j0:j1].bitcast(FP8X4),
@@ -94,7 +106,7 @@ def tile_picked_place_lin_none_srt_l_kernel(tc, xT, w, gate, offs, out):
                 start=True,
                 stop=True,
             )
-            nc.scalar.copy(out=ys[m][:, j0:j1], in_=acc[:, 0 : j1 - j0])
+            nc.scalar.copy(out=ys[m][:, j0:j1], in_=acc)
 
         def scatter(m, j0, j1):
             nc.vector.tensor_tensor(
@@ -104,41 +116,48 @@ def tile_picked_place_lin_none_srt_l_kernel(tc, xT, w, gate, offs, out):
         def store(m):
             nc.sync.dma_start(out=out[m * P : (m + 1) * P, :], in_=windows[m][:])
 
-        interleave(nc.scalar.copy, w_grp[0][:], w_raw[0][:])
-        interleave(nc.vector.tensor_copy, x_grp[0][:], x_raw[0][:])
+        act, dve = nc.scalar.copy, nc.vector.tensor_copy
+
+        group(act, w_grp[0], w_raw[0], 0, 128)
         quantise_w(0)
+        group(act, x_grp[0], x_raw[0], 176, 256)
+        group(dve, x_grp[0], x_raw[0], 0, 176)
         quantise_x(0)
-        product(0, 0, Q, 0)
-        product(1, 0, Q, 1)
-        interleave(nc.vector.tensor_copy, x_grp[1][:], x_raw[1][:])
-        scatter(0, 0, Q)
-        quantise_x(1)
-        product(0, Q, 2 * Q, 2)
-        product(1, Q, 2 * Q, 3)
-        interleave(nc.scalar.copy, x_grp[2][:], x_raw[2][:])
-        scatter(1, 0, Q)
-        quantise_x(2)
-        product(0, 2 * Q, 3 * Q, 4)
-        product(1, 2 * Q, 3 * Q, 5)
-        interleave(nc.scalar.copy, x_grp[3][:], x_raw[3][:])
-        scatter(0, Q, 2 * Q)
-        scatter(1, Q, 2 * Q)
-        quantise_x(3)
-        product(0, 3 * Q, S, 6)
-        product(1, 3 * Q, S, 7)
-        interleave(nc.scalar.copy, w_grp[1][:], w_raw[1][:])
-        scatter(0, 2 * Q, 3 * Q)
-        scatter(1, 2 * Q, 3 * Q)
+        product(0, 0, 256)
+        group(dve, w_grp[1], w_raw[1], 0, 128)
         quantise_w(1)
-        scatter(0, 3 * Q, S)
+        product(1, 0, 256)
+        scatter(0, 0, 256)
+        group(act, x_grp[1], x_raw[1], 128, 256)
+        group(dve, x_grp[1], x_raw[1], 0, 128)
+        quantise_x(1)
+        product(0, 256, 512)
+        product(1, 256, 512)
+        scatter(1, 0, 256)
+        group(act, w_grp[2], w_raw[2], 0, 256)
+        scatter(0, 256, 512)
+        quantise_w(2)
+        product(2, 0, 512)
+        scatter(1, 256, 512)
+        group(act, x_grp[2], x_raw[2], 0, 256)
+        scatter(2, 0, 256)
+        quantise_x(2)
+        product(0, 512, 768)
+        group(act, x_grp[3], x_raw[3], 0, 256)
+        scatter(2, 256, 512)
+        quantise_x(3)
+        product(0, 768, 1024)
+        scatter(0, 512, 768)
+        product(1, 512, 1024)
+        scatter(0, 768, 1024)
         store(0)
-        product(2, 0, 512, 0)
-        product(2, 512, S, 1)
-        scatter(1, 3 * Q, S)
+        product(2, 512, 1024)
+        scatter(1, 512, 1024)
         store(1)
-        product(3, 0, 512, 2)
-        product(3, 512, S, 3)
-        scatter(2, 0, S)
+        product(3, 0, 512)
+        product(3, 512, 1024)
+        scatter(2, 512, 1024)
         store(2)
-        scatter(3, 0, S)
-        store(3)
+        scatter(3, 0, 1024)
+        nc.sync.dma_start(out=out[3 * P : 4 * P, 0:1024], in_=windows[3][:, 0:1024])
+        nc.scalar.dma_start(out=out[3 * P : 4 * P, 1024:2048], in_=windows[3][:, 1024:2048])

from contextlib import ExitStack

import concourse.mybir as mybir

K, T, S, N = 512, 2048, 1024, 512
P = 128
PACK = 4
FLOPS = 2 * K * S * N
BYTES = 4 * (K * S + K * N + S + N * T) + 2 * S

F32 = mybir.dt.float32
BF16 = mybir.dt.bfloat16
U32 = mybir.dt.uint32
U16 = mybir.dt.uint16
U8 = mybir.dt.uint8
FP8X4 = mybir.dt.float8_e4m3fn_x4
MULT = mybir.AluOpType.mult


def interleave(copy, dst, src):
    copy(
        out=dst.rearrange("p (c i j) -> p c j i", i=4, j=PACK),
        in_=src.rearrange("p j (c i) -> p c j i", i=4),
    )


def tile_picked_place_lin_none_srt_l_kernel(tc, xT, w, gate, offs, out):
    nc = tc.nc
    x_rows = xT.rearrange("(p j) s -> p j s", j=PACK)
    w_rows = w.rearrange("(p j) n -> p j n", j=PACK)

    with ExitStack() as ctx:
        keep = ctx.enter_context(tc.tile_pool(name="keep", bufs=1))
        psum = ctx.enter_context(tc.psum_pool(name="psum", bufs=1))

        x_cuts = [(0, 256), (256, 512), (512, 768), (768, 1024)]
        w_cuts = [(0, 128), (128, 256), (256, 512)]
        offsets = keep.tile([P, S // 16], U16, name="offsets")
        gates = keep.tile([P, S], F32, name="gates", align_bytes=64)
        x_raw = [keep.tile([P, PACK, b - a], F32, name=f"x_raw{a}") for a, b in x_cuts]
        w_raw = [keep.tile([P, PACK, b - a], F32, name=f"w_raw{a}") for a, b in w_cuts]
        x_grp = [keep.tile([P, PACK * (b - a)], BF16, name=f"x_grp{a}", align_bytes=64) for a, b in x_cuts]
        w_grp = [keep.tile([P, PACK * (b - a)], BF16, name=f"w_grp{a}", align_bytes=64) for a, b in w_cuts]
        x_codes = keep.tile([P, S], U32, name="x_codes", align_bytes=64)
        x_scales = keep.tile([P, S], U8, name="x_scales", align_bytes=64)
        w_codes = keep.tile([P, N], U32, name="w_codes", align_bytes=64)
        w_scales = keep.tile([P, N], U8, name="w_scales", align_bytes=64)
        windows = [keep.tile([P, T], F32, name=f"window{m}") for m in range(4)]
        ys = [keep.tile([P, S], F32, name=f"y{m}", align_bytes=64) for m in range(4)]
        zero = keep.tile([P, 8], F32, name="zero")

        def load_x(i):
            a, b = x_cuts[i]
            nc.sync.dma_start(out=x_raw[i][:], in_=x_rows[:, :, a:b])

        def load_w(i):
            a, b = w_cuts[i]
            nc.sync.dma_start(out=w_raw[i][:], in_=w_rows[:, :, a:b])

        def load_gate(a, b):
            nc.sync.dma_start(out=gates[:, a:b], in_=gate[0:P, a:b])

        load_w(0)
        load_x(0)
        nc.sync.dma_start(offsets[:], offs)
        load_gate(0, 256)
        load_w(1)
        load_x(1)
        load_w(2)
        load_gate(256, 1024)
        load_x(2)
        load_x(3)

        nc.vector.memset(zero[:], 0.0)
        for m in range(3):
            nc.vector.memset(windows[m][:], 0.0)
        nc.scalar.copy(out=windows[3][:], in_=zero[:, 0:1].to_broadcast([P, T]))

        def group(copy, grp, raw, a, b):
            interleave(copy, grp[:, PACK * a : PACK * b], raw[:, :, a:b])

        def quantise_w(i):
            a, b = w_cuts[i]
            nc.vector.quantize_mx(
                out=w_codes[:, a:b].bitcast(FP8X4), scales=w_scales[:, a:b], in_=w_grp[i][:]
            )

        def quantise_x(i):
            a, b = x_cuts[i]
            nc.vector.quantize_mx(
                out=x_codes[:, a:b].bitcast(FP8X4), scales=x_scales[:, a:b], in_=x_grp[i][:]
            )

        banks = [psum.tile([P, 512], F32, name=f"bank{b}") for b in range(8)]
        free = list(range(11))

        def product(m, j0, j1):
            acc = banks[free[0] % 8][:, 0 : j1 - j0]
            free.remove(free[0])
            nc.tensor.matmul_mx(
                out=acc,
                lhsT=w_codes[:, m * P : (m + 1) * P].bitcast(FP8X4),
                lhsT_scale=w_scales[:, m * P : (m + 1) * P],
                rhs=x_codes[:, j0:j1].bitcast(FP8X4),
                rhs_scale=x_scales[:, j0:j1],
                start=True,
                stop=True,
            )
            nc.scalar.copy(out=ys[m][:, j0:j1], in_=acc)

        def scatter(m, j0, j1):
            nc.vector.tensor_tensor(
                windows[m][:].indirect(offsets[:, j0 // 16 : j1 // 16]), ys[m][:, j0:j1], gates[:, j0:j1], MULT
            )

        def store(m):
            nc.sync.dma_start(out=out[m * P : (m + 1) * P, :], in_=windows[m][:])

        act, dve = nc.scalar.copy, nc.vector.tensor_copy

        group(act, w_grp[0], w_raw[0], 0, 128)
        quantise_w(0)
        group(act, x_grp[0], x_raw[0], 176, 256)
        group(dve, x_grp[0], x_raw[0], 0, 176)
        quantise_x(0)
        product(0, 0, 256)
        group(dve, w_grp[1], w_raw[1], 0, 128)
        quantise_w(1)
        product(1, 0, 256)
        scatter(0, 0, 256)
        group(act, x_grp[1], x_raw[1], 128, 256)
        group(dve, x_grp[1], x_raw[1], 0, 128)
        quantise_x(1)
        product(0, 256, 512)
        product(1, 256, 512)
        scatter(1, 0, 256)
        group(act, w_grp[2], w_raw[2], 0, 256)
        scatter(0, 256, 512)
        quantise_w(2)
        product(2, 0, 512)
        scatter(1, 256, 512)
        group(act, x_grp[2], x_raw[2], 0, 256)
        scatter(2, 0, 256)
        quantise_x(2)
        product(0, 512, 768)
        group(act, x_grp[3], x_raw[3], 0, 256)
        scatter(2, 256, 512)
        quantise_x(3)
        product(0, 768, 1024)
        scatter(0, 512, 768)
        product(1, 512, 1024)
        scatter(0, 768, 1024)
        store(0)
        product(2, 512, 1024)
        scatter(1, 512, 1024)
        store(1)
        product(3, 0, 512)
        product(3, 512, 1024)
        scatter(2, 512, 1024)
        store(2)
        scatter(3, 0, 1024)
        nc.sync.dma_start(out=out[3 * P : 4 * P, 0:1024], in_=windows[3][:, 0:1024])
        nc.scalar.dma_start(out=out[3 * P : 4 * P, 1024:2048], in_=windows[3][:, 1024:2048])
